import numpy as np
import ml_dtypes


def mxq(x, axis, fmt="e4m3"):
    dtype, down = {"e4m3": (ml_dtypes.float8_e4m3fn, 7), "e5m2": (ml_dtypes.float8_e5m2, 14)}[fmt]
    v = np.moveaxis(np.asarray(x, np.float32).astype(ml_dtypes.bfloat16).astype(np.float64), axis, -1)
    blocks = v.reshape(v.shape[:-1] + (-1, 32))
    amax = np.abs(blocks).max(-1, keepdims=True)
    byte = np.maximum(np.where(amax > 0, np.frexp(amax)[1] - 1 + 127, 0) - down, 1)
    scale = np.exp2(byte - 127.0)
    codes = (blocks / scale).astype(np.float32).astype(dtype).astype(np.float64)
    return np.moveaxis((codes * scale).reshape(v.shape), -1, axis)


WIDE = False


def mx_kscale(k):
    if not WIDE:
        return np.ones(k)
    levels = np.array([10, -10, 5, -5, 0])
    if k % 512:
        return np.exp2(np.random.permutation(np.resize(levels, k // 32))).repeat(32)
    a = np.empty((k // 512, 16))
    for p in range(k // 512):
        a[p, :8] = np.random.permutation(np.resize(levels, 8))
        for g in range(8):
            far = levels[np.abs(levels - a[p, g]) >= 10]
            a[p, g + 8] = far[np.random.randint(len(far))]
    return np.exp2(a.ravel()).repeat(32)


def f64(x):
    return np.asarray(x).astype(np.float64)


def striped(idx):
    return np.tile(idx.reshape(-1, 16).T, (8, 1)).astype(np.uint16)


def unstriped(offs):
    return offs[:16].T.reshape(-1).astype(np.int64)


def striped8(idx):
    return np.concatenate([x.reshape(-1, 16).T for x in idx]).astype(np.uint16)


def runs(offs, k):
    lists = np.stack([offs[16 * r : 16 * r + 16].T.reshape(-1) for r in range(8)]).astype(np.int64)
    return lists[np.arange(k) % 512 // 64]


def pack_weight(w):
    k, n = w.shape
    w = f64(np.asarray(w, np.float32).astype(ml_dtypes.bfloat16)).reshape(k // 32, 32, n)
    amax = np.abs(w).max(1)
    byte = np.clip(np.where(amax > 0, np.frexp(amax)[1] - 1 + 127 - 7, 1), 1, 254)
    scaled = (w * np.exp2(127.0 - byte)[:, None, :]).reshape(k, n).astype(np.float32)
    words = np.ascontiguousarray(scaled.reshape(k // 512, 128, 4, n).transpose(0, 1, 3, 2)).astype(ml_dtypes.float8_e4m3fn).view(np.uint8)
    return words, np.ascontiguousarray(byte.astype(np.uint8).reshape(k // 512, 16, n))


def unpack_weight(words, scales):
    g, p, n, _ = words.shape
    vals = np.ascontiguousarray(words).view(ml_dtypes.float8_e4m3fn).astype(np.float64) * np.repeat(np.exp2(scales.astype(np.float64) - 127.0), 8, axis=1)[..., None]
    return vals.transpose(0, 1, 3, 2).reshape(g * 512, n)


K, T, S, N, H = 512, 2048, 512, 512, 512


def setup_inputs():
    n = np.random.standard_normal
    s = mx_kscale(K)[:, None]
    u = mx_kscale(H)
    packed_xT = pack_weight(n((K, T)) * s)
    return {
        "x_words": packed_xT[0],
        "x_scales": packed_xT[1],
        "w1": (n((K, H)) / np.sqrt(K) / s).astype(np.float32),
        "gn": (np.random.uniform(0.5, 1.5, (H, 1)) * u[:, None]).astype(np.float32),
        "w2": (n((H, N)) / np.sqrt(H) / u[:, None]).astype(np.float32),
        "offs": striped(np.random.permutation(T)[:S]),
        "n1": striped8(np.stack([np.random.permutation(S) for _ in range(8)])),
        "n2": striped8(np.stack([np.random.permutation(S) for _ in range(8)])),
        "n3": striped8(np.stack([np.random.permutation(S) for _ in range(8)])),
    }


def reference(x_words, x_scales, w1, gn, w2, offs, n1, n2, n3):
    xq = unpack_weight(x_words, x_scales)[:, unstriped(offs)]
    y = mxq(f64(w1), 0, "e4m3").T @ xq
    z = f64(gn) * (np.exp(-1.0 * (np.abs(y[np.arange(H)[:, None], runs(n1, H)] - (y[np.arange(H)[:, None], runs(n2, H)])))))
    h = mxq(f64(w2), 0, "e4m3").T @ mxq(z, 0, "e4m3")
    a = h[np.arange(N)[:, None], runs(n3, N)]
    return (h * a) / ((a) ** 2 + 0.5)

@@ -1,0 +1,170 @@
+from contextlib import ExitStack
+
+import concourse.mybir as mybir
+
+K, T, S, H, N = 512, 2048, 512, 512, 512
+FLOPS = 2 * K * H * S + 2 * H * N * S
+
+F32 = mybir.dt.float32
+BF16 = mybir.dt.bfloat16
+I32 = mybir.dt.int32
+U32 = mybir.dt.uint32
+U16 = mybir.dt.uint16
+U8 = mybir.dt.uint8
+FP8X4 = mybir.dt.float8_e4m3fn_x4
+ACT = mybir.ActivationFunctionType
+ALU = mybir.AluOpType
+
+P = 128
+PACK = 4
+HALF = S // 2
+PER_COL = 16
+W1_VECTOR_M = 80
+
+
+def tile_picked_laplace8_none_p_kernel(tc, x_words, x_scales, w1, gn, w2, offs, n1, n2, n3, out):
+    nc = tc.nc
+    with ExitStack() as ctx:
+        keep = ctx.enter_context(tc.tile_pool(name="keep", bufs=1))
+        psum = ctx.enter_context(tc.psum_pool(name="psum", bufs=1))
+
+        def sb(name, shape, dtype):
+            return keep.tile(shape, dtype, name=name, align_bytes=64)
+
+        offs_sb = keep.tile([P, S // PER_COL], U16, name="offs_sb")
+        n1_sb = keep.tile([P, S // PER_COL], U16, name="n1_sb")
+        n2_sb = keep.tile([P, S // PER_COL], U16, name="n2_sb")
+        n3_sb = keep.tile([P, S // PER_COL], U16, name="n3_sb")
+        xs_all = sb("xs_all", [P, T], U8)
+        xs_rows = sb("xs_rows", [P, T // 4], I32)
+        xw_all = sb("xw_all", [P, T], I32)
+        w1_raw = sb("w1_raw", [P, PACK, H], F32)
+        w2_raw = sb("w2_raw", [P, PACK, N], F32)
+        gn_sb = sb("gn_sb", [P, PACK], F32)
+
+        nc.vector.memset(xs_all[:].bitcast(I32), 0)
+        nc.sync.dma_start(offs_sb[:], offs)
+        for q in range(4):
+            nc.scalar.dma_start(out=xs_rows[32 * q : 32 * q + 4, :], in_=x_scales[0, 4 * q : 4 * q + 4, :].bitcast(I32))
+        nc.sync.dma_start(out=w1_raw[:], in_=w1.rearrange("(p j) c -> p j c", j=PACK))
+        nc.sync.dma_start(out=xw_all[:], in_=x_words[0].rearrange("p c r -> p (c r)").bitcast(I32))
+        nc.sync.dma_start(n1_sb[:], n1)
+        nc.sync.dma_start(n2_sb[:], n2)
+        nc.sync.dma_start(out=w2_raw[:], in_=w2.rearrange("(p j) c -> p j c", j=PACK))
+        nc.sync.dma_start(out=gn_sb[:], in_=gn.rearrange("(p t) o -> p (t o)", t=PACK))
+        nc.sync.dma_start(n3_sb[:], n3)
+
+        def halves(tile, h):
+            return tile[:, h * (HALF // PER_COL) : (h + 1) * (HALF // PER_COL)]
+
+        def cols(h):
+            return slice(h * HALF, (h + 1) * HALF)
+
+        xs = sb("xs", [P, S], U8)
+        for q in range(4):
+            nc.vector.tensor_copy(out=xs_all[32 * q : 32 * q + 4, :].bitcast(I32), in_=xs_rows[32 * q : 32 * q + 4, :])
+        nc.vector.tensor_copy(xs[:], xs_all[:].indirect(offs_sb[:]))
+
+        def deal(raw, grouped, vector_m):
+            src = raw[:].rearrange("p j (m t) -> p m t j", t=PACK)
+            dst = grouped[:].rearrange("p t m j -> p m t j")
+            if vector_m > 0:
+                nc.vector.tensor_copy(out=dst[:, :vector_m], in_=src[:, :vector_m])
+            nc.scalar.copy(out=dst[:, vector_m:], in_=src[:, vector_m:])
+
+        def quantize(grouped_flat, codes, scales):
+            nc.vector.quantize_mx(out=codes.bitcast(FP8X4), scales=scales, in_=grouped_flat)
+
+        w1_g = sb("w1_g", [P, PACK, P, PACK], BF16)
+        w1_c = sb("w1_c", [P, H], U32)
+        w1_s = sb("w1_s", [P, H], U8)
+        deal(w1_raw, w1_g, W1_VECTOR_M)
+        quantize(w1_g[:].rearrange("p t m j -> p (t m j)"), w1_c[:], w1_s[:])
+
+        xw = [sb("xw%d" % h, [P, HALF], U32) for h in range(2)]
+        for h in range(2):
+            nc.vector.tensor_copy(xw[h][:], xw_all[:].bitcast(U32).indirect(halves(offs_sb, h)))
+
+        y = [sb("y%d" % t, [P, S], F32) for t in range(PACK)]
+        for t in range(PACK):
+            for h in range(2):
+                bank = psum.tile([P, HALF], F32, name="ybank%d_%d" % (h, t), tag="bank%d" % (4 * h + t))
+                nc.tensor.matmul_mx(
+                    out=bank[:],
+                    lhsT=w1_c[:, t * P : (t + 1) * P].bitcast(FP8X4),
+                    lhsT_scale=w1_s[:, t * P : (t + 1) * P],
+                    rhs=xw[h][:].bitcast(FP8X4),
+                    rhs_scale=xs[:, cols(h)],
+                    start=True,
+                    stop=True,
+                )
+                nc.scalar.copy(out=y[t][:, cols(h)], in_=bank[:])
+
+        w2_g = sb("w2_g", [P, PACK, P, PACK], BF16)
+        w2_c = sb("w2_c", [P, N], U32)
+        w2_s = sb("w2_s", [P, N], U8)
+        deal(w2_raw, w2_g, 0)
+
+        e = [sb("e%d" % h, [P, PACK, HALF], F32) for h in range(2)]
+        for h in range(2):
+            first = sb("first%d" % h, [P, PACK, HALF], F32)
+            diff = sb("diff%d" % h, [P, PACK, HALF], F32)
+            dist = sb("dist%d" % h, [P, PACK, HALF], F32)
+            for pair in range(2):
+                for t in (2 * pair, 2 * pair + 1):
+                    nc.vector.tensor_copy(first[:, t, :], y[t][:].indirect(halves(n2_sb, h)))
+                for t in (2 * pair, 2 * pair + 1):
+                    nc.vector.tensor_tensor(diff[:, t, :], y[t][:].indirect(halves(n1_sb, h)), first[:, t, :], ALU.subtract)
+                for t in (2 * pair, 2 * pair + 1):
+                    nc.scalar.activation(dist[:, t, :], diff[:, t, :], ACT.Abs)
+                for t in (2 * pair, 2 * pair + 1):
+                    nc.scalar.activation(e[h][:, t, :], dist[:, t, :], ACT.Exp, scale=-1.0)
+
+        quantize(w2_g[:].rearrange("p t m j -> p (t m j)"), w2_c[:], w2_s[:])
+
+        hid = [sb("hid%d" % t, [P, S], F32) for t in range(PACK)]
+        sq = [sb("sq%d" % t, [P, S], F32) for t in range(PACK)]
+        gain = gn_sb[:].unsqueeze(1).unsqueeze(3).to_broadcast([P, HALF // 4, PACK, 4])
+        hbanks = {}
+        for h in range(2):
+            z = sb("z%d" % h, [P, HALF, PACK], BF16)
+            z_c = sb("z_c%d" % h, [P, HALF], U32)
+            z_s = sb("z_s%d" % h, [P, HALF], U8)
+            nc.vector.tensor_tensor(
+                z[:].rearrange("p (c i) t -> p c t i", i=4), e[h][:].rearrange("p t (c i) -> p c t i", i=4), gain, ALU.mult
+            )
+            quantize(z[:].rearrange("p j t -> p (j t)"), z_c[:], z_s[:])
+            for t in range(PACK):
+                bank = psum.tile([P, HALF], F32, name="hbank%d_%d" % (h, t), tag="bank%d" % (4 * h + t))
+                nc.tensor.matmul_mx(
+                    out=bank[:],
+                    lhsT=w2_c[:, t * P : (t + 1) * P].bitcast(FP8X4),
+                    lhsT_scale=w2_s[:, t * P : (t + 1) * P],
+                    rhs=z_c[:].bitcast(FP8X4),
+                    rhs_scale=z_s[:],
+                    start=True,
+                    stop=True,
+                )
+                hbanks[(h, t)] = bank
+
+        out_rows = out.rearrange("(p t) n -> p t n", t=PACK)
+        for t in range(PACK):
+            root = sb("root%d" % t, [P, S], F32)
+            inv = sb("inv%d" % t, [P, S], F32)
+            f = sb("f%d" % t, [P, S], F32)
+            res = sb("res%d" % t, [P, S], F32)
+            for h in range(2):
+                nc.scalar.activation(sq[t][:, cols(h)], hbanks[(h, t)][:], ACT.Square)
+                if h == 0 or t == 0:
+                    nc.vector.tensor_copy(out=hid[t][:, cols(h)], in_=hbanks[(h, t)][:])
+            for h in range(2):
+                nc.scalar.activation(root[:, cols(h)], sq[t][:, cols(h)], ACT.Abs_reciprocal_sqrt, bias=0.5)
+            for h in range(2):
+                nc.scalar.activation(inv[:, cols(h)], root[:, cols(h)], ACT.Square)
+            if t > 0:
+                nc.scalar.copy(out=hid[t][:, cols(1)], in_=hbanks[(1, t)][:])
+            for h in range(2):
+                nc.vector.tensor_tensor(f[:, cols(h)], hbanks[(h, t)][:], inv[:, cols(h)], ALU.mult)
+            for h in range(2):
+                nc.vector.tensor_tensor(res[:, cols(h)], f[:].indirect(halves(n3_sb, h)), hid[t][:, cols(h)], ALU.mult)
+                nc.sync.dma_start(out=out_rows[:, t, cols(h)], in_=res[:, cols(h)])

@@ -18,8 +18,9 @@ ALU = mybir.AluOpType
 P = 128
 PACK = 4
 HALF = S // 2
+QUARTER = S // 4
 PER_COL = 16
-W1_VECTOR_M = 80
+W1_VECTOR_M = 56
 
 
 def tile_picked_laplace8_none_p_kernel(tc, x_words, x_scales, w1, gn, w2, offs, n1, n2, n3, out):
@@ -28,15 +29,14 @@ def tile_picked_laplace8_none_p_kernel(tc, x_words, x_scales, w1, gn, w2, offs, 
         keep = ctx.enter_context(tc.tile_pool(name="keep", bufs=1))
         psum = ctx.enter_context(tc.psum_pool(name="psum", bufs=1))
 
-        def sb(name, shape, dtype):
-            return keep.tile(shape, dtype, name=name, align_bytes=64)
+        def sb(name, shape, dtype, tag=None):
+            return keep.tile(shape, dtype, name=name, tag=tag or name, align_bytes=64)
 
         offs_sb = keep.tile([P, S // PER_COL], U16, name="offs_sb")
         n1_sb = keep.tile([P, S // PER_COL], U16, name="n1_sb")
         n2_sb = keep.tile([P, S // PER_COL], U16, name="n2_sb")
         n3_sb = keep.tile([P, S // PER_COL], U16, name="n3_sb")
         xs_all = sb("xs_all", [P, T], U8)
-        xs_rows = sb("xs_rows", [P, T // 4], I32)
         xw_all = sb("xw_all", [P, T], I32)
         w1_raw = sb("w1_raw", [P, PACK, H], F32)
         w2_raw = sb("w2_raw", [P, PACK, N], F32)
@@ -44,12 +44,12 @@ def tile_picked_laplace8_none_p_kernel(tc, x_words, x_scales, w1, gn, w2, offs, 
 
         nc.vector.memset(xs_all[:].bitcast(I32), 0)
         nc.sync.dma_start(offs_sb[:], offs)
-        for q in range(4):
-            nc.scalar.dma_start(out=xs_rows[32 * q : 32 * q + 4, :], in_=x_scales[0, 4 * q : 4 * q + 4, :].bitcast(I32))
         nc.sync.dma_start(out=w1_raw[:], in_=w1.rearrange("(p j) c -> p j c", j=PACK))
+        for q in range(4):
+            nc.sync.dma_start(out=xs_all[32 * q : 32 * q + 4, :].bitcast(I32), in_=x_scales[0, 4 * q : 4 * q + 4, :].bitcast(I32))
         nc.sync.dma_start(out=xw_all[:], in_=x_words[0].rearrange("p c r -> p (c r)").bitcast(I32))
-        nc.sync.dma_start(n1_sb[:], n1)
         nc.sync.dma_start(n2_sb[:], n2)
+        nc.sync.dma_start(n1_sb[:], n1)
         nc.sync.dma_start(out=w2_raw[:], in_=w2.rearrange("(p j) c -> p j c", j=PACK))
         nc.sync.dma_start(out=gn_sb[:], in_=gn.rearrange("(p t) o -> p (t o)", t=PACK))
         nc.sync.dma_start(n3_sb[:], n3)
@@ -60,14 +60,9 @@ def tile_picked_laplace8_none_p_kernel(tc, x_words, x_scales, w1, gn, w2, offs, 
         def cols(h):
             return slice(h * HALF, (h + 1) * HALF)
 
-        xs = sb("xs", [P, S], U8)
-        for q in range(4):
-            nc.vector.tensor_copy(out=xs_all[32 * q : 32 * q + 4, :].bitcast(I32), in_=xs_rows[32 * q : 32 * q + 4, :])
-        nc.vector.tensor_copy(xs[:], xs_all[:].indirect(offs_sb[:]))
-
         def deal(raw, grouped, vector_m):
-            src = raw[:].rearrange("p j (m t) -> p m t j", t=PACK)
-            dst = grouped[:].rearrange("p t m j -> p m t j")
+            src = raw[:].rearrange("p j (m t) -> p m j t", t=PACK)
+            dst = grouped[:].rearrange("p t m j -> p m j t")
             if vector_m > 0:
                 nc.vector.tensor_copy(out=dst[:, :vector_m], in_=src[:, :vector_m])
             nc.scalar.copy(out=dst[:, vector_m:], in_=src[:, vector_m:])
@@ -75,10 +70,23 @@ def tile_picked_laplace8_none_p_kernel(tc, x_words, x_scales, w1, gn, w2, offs, 
         def quantize(grouped_flat, codes, scales):
             nc.vector.quantize_mx(out=codes.bitcast(FP8X4), scales=scales, in_=grouped_flat)
 
+        def product(dst, w_c, w_s, t, rhs_c, rhs_s):
+            nc.tensor.matmul_mx(
+                out=dst,
+                lhsT=w_c[:, t * P : (t + 1) * P].bitcast(FP8X4),
+                lhsT_scale=w_s[:, t * P : (t + 1) * P],
+                rhs=rhs_c.bitcast(FP8X4),
+                rhs_scale=rhs_s,
+                start=True,
+                stop=True,
+            )
+
         w1_g = sb("w1_g", [P, PACK, P, PACK], BF16)
         w1_c = sb("w1_c", [P, H], U32)
         w1_s = sb("w1_s", [P, H], U8)
         deal(w1_raw, w1_g, W1_VECTOR_M)
+        xs = sb("xs", [P, S], U8)
+        nc.vector.tensor_copy(xs[:], xs_all[:].indirect(offs_sb[:]))
         quantize(w1_g[:].rearrange("p t m j -> p (t m j)"), w1_c[:], w1_s[:])
 
         xw = [sb("xw%d" % h, [P, HALF], U32) for h in range(2)]
@@ -86,85 +94,97 @@ def tile_picked_laplace8_none_p_kernel(tc, x_words, x_scales, w1, gn, w2, offs, 
             nc.vector.tensor_copy(xw[h][:], xw_all[:].bitcast(U32).indirect(halves(offs_sb, h)))
 
         y = [sb("y%d" % t, [P, S], F32) for t in range(PACK)]
-        for t in range(PACK):
-            for h in range(2):
+        for pair in range(2):
+            for h, t in ((0, 2 * pair), (0, 2 * pair + 1), (1, 2 * pair), (1, 2 * pair + 1)):
                 bank = psum.tile([P, HALF], F32, name="ybank%d_%d" % (h, t), tag="bank%d" % (4 * h + t))
-                nc.tensor.matmul_mx(
-                    out=bank[:],
-                    lhsT=w1_c[:, t * P : (t + 1) * P].bitcast(FP8X4),
-                    lhsT_scale=w1_s[:, t * P : (t + 1) * P],
-                    rhs=xw[h][:].bitcast(FP8X4),
-                    rhs_scale=xs[:, cols(h)],
-                    start=True,
-                    stop=True,
-                )
+                product(bank[:], w1_c, w1_s, t, xw[h][:], xs[:, cols(h)])
                 nc.scalar.copy(out=y[t][:, cols(h)], in_=bank[:])
 
         w2_g = sb("w2_g", [P, PACK, P, PACK], BF16)
-        w2_c = sb("w2_c", [P, N], U32)
         w2_s = sb("w2_s", [P, N], U8)
         deal(w2_raw, w2_g, 0)
 
-        e = [sb("e%d" % h, [P, PACK, HALF], F32) for h in range(2)]
-        for h in range(2):
-            first = sb("first%d" % h, [P, PACK, HALF], F32)
-            diff = sb("diff%d" % h, [P, PACK, HALF], F32)
-            dist = sb("dist%d" % h, [P, PACK, HALF], F32)
-            for pair in range(2):
-                for t in (2 * pair, 2 * pair + 1):
-                    nc.vector.tensor_copy(first[:, t, :], y[t][:].indirect(halves(n2_sb, h)))
-                for t in (2 * pair, 2 * pair + 1):
-                    nc.vector.tensor_tensor(diff[:, t, :], y[t][:].indirect(halves(n1_sb, h)), first[:, t, :], ALU.subtract)
-                for t in (2 * pair, 2 * pair + 1):
-                    nc.scalar.activation(dist[:, t, :], diff[:, t, :], ACT.Abs)
-                for t in (2 * pair, 2 * pair + 1):
-                    nc.scalar.activation(e[h][:, t, :], dist[:, t, :], ACT.Exp, scale=-1.0)
+        e = [sb("e%d" % h, [P, 2, PACK, QUARTER], F32) for h in range(2)]
+        zt = [sb("zt%d" % h, [P, 2, PACK, QUARTER], BF16) for h in range(2)]
+        for t in range(PACK):
+            first = [sb("first%d_%d" % (t, h), [P, HALF], F32) for h in range(2)]
+            diff = sb("diff%d" % t, [P, S], F32)
+            dist = sb("dist%d" % t, [P, S], F32)
+            for h in range(2):
+                nc.vector.tensor_copy(first[h][:], y[t][:].indirect(halves(n2_sb, h)))
+            for h in range(2):
+                nc.vector.tensor_tensor(diff[:, cols(h)], y[t][:].indirect(halves(n1_sb, h)), first[h][:], ALU.subtract)
+            for h in range(2):
+                nc.scalar.activation(dist[:, cols(h)], diff[:, cols(h)], ACT.Abs)
+                nc.scalar.activation(e[h][:, :, t, :], dist[:, cols(h)].rearrange("p (c n) -> p c n", c=2), ACT.Exp, scale=-1.0)
+                if h in (1,):
+                    nc.scalar.activation(zt[h][:, :, t, :], e[h][:, :, t, :], ACT.Copy, scale=gn_sb[:, t : t + 1])
 
+        w2_c = sb("w2_c", [P, N], U32, tag="first3_0")
         quantize(w2_g[:].rearrange("p t m j -> p (t m j)"), w2_c[:], w2_s[:])
+        warm = sb("warm", [P, 1], F32)
+        nc.scalar.activation(warm[:], zt[1][:, 1, PACK - 1, 0:1], ACT.Abs_reciprocal_sqrt, bias=0.5)
 
-        hid = [sb("hid%d" % t, [P, S], F32) for t in range(PACK)]
-        sq = [sb("sq%d" % t, [P, S], F32) for t in range(PACK)]
-        gain = gn_sb[:].unsqueeze(1).unsqueeze(3).to_broadcast([P, HALF // 4, PACK, 4])
+        gain = gn_sb[:].unsqueeze(1).unsqueeze(3).to_broadcast([P, QUARTER // 4, PACK, 4])
         hbanks = {}
         for h in range(2):
-            z = sb("z%d" % h, [P, HALF, PACK], BF16)
+            z = [sb("z%d_%d" % (h, c), [P, QUARTER, PACK], BF16) for c in range(2)]
             z_c = sb("z_c%d" % h, [P, HALF], U32)
             z_s = sb("z_s%d" % h, [P, HALF], U8)
-            nc.vector.tensor_tensor(
-                z[:].rearrange("p (c i) t -> p c t i", i=4), e[h][:].rearrange("p t (c i) -> p c t i", i=4), gain, ALU.mult
-            )
-            quantize(z[:].rearrange("p j t -> p (j t)"), z_c[:], z_s[:])
+            for c in range(2):
+                if h in (1,):
+                    nc.vector.tensor_copy(
+                        out=z[c][:].rearrange("p (a i) t -> p a t i", i=4), in_=zt[h][:, c].rearrange("p t (a i) -> p a t i", i=4)
+                    )
+                    continue
+                nc.vector.tensor_tensor(
+                    z[c][:].rearrange("p (a i) t -> p a t i", i=4),
+                    e[h][:, c].rearrange("p t (a i) -> p a t i", i=4),
+                    gain,
+                    ALU.mult,
+                )
+            for c in range(2):
+                q = slice(c * QUARTER, (c + 1) * QUARTER)
+                quantize(z[c][:].rearrange("p j t -> p (j t)"), z_c[:, q], z_s[:, q])
             for t in range(PACK):
                 bank = psum.tile([P, HALF], F32, name="hbank%d_%d" % (h, t), tag="bank%d" % (4 * h + t))
-                nc.tensor.matmul_mx(
-                    out=bank[:],
-                    lhsT=w2_c[:, t * P : (t + 1) * P].bitcast(FP8X4),
-                    lhsT_scale=w2_s[:, t * P : (t + 1) * P],
-                    rhs=z_c[:].bitcast(FP8X4),
-                    rhs_scale=z_s[:],
-                    start=True,
-                    stop=True,
-                )
+                for c in range(2):
+                    q = slice(c * QUARTER, (c + 1) * QUARTER)
+                    product(bank[:, q], w2_c, w2_s, t, z_c[:, q], z_s[:, q])
                 hbanks[(h, t)] = bank
 
+        fs = []
         out_rows = out.rearrange("(p t) n -> p t n", t=PACK)
         for t in range(PACK):
+            hid = sb("hid%d" % t, [P, S], F32)
+            sq = sb("sq%d" % t, [P, S], F32)
             root = sb("root%d" % t, [P, S], F32)
-            inv = sb("inv%d" % t, [P, S], F32)
-            f = sb("f%d" % t, [P, S], F32)
+            window = sb("window%d" % t, [P, 2 * S], F32)
+            f = window[:, :S]
+            inv = window[:, S:]
+            fs.append(f)
             res = sb("res%d" % t, [P, S], F32)
             for h in range(2):
-                nc.scalar.activation(sq[t][:, cols(h)], hbanks[(h, t)][:], ACT.Square)
-                if h == 0 or t == 0:
-                    nc.vector.tensor_copy(out=hid[t][:, cols(h)], in_=hbanks[(h, t)][:])
+                if t > 0 and not (h, t) in ((1,3,),):
+                    nc.vector.tensor_copy(out=hid[:, cols(h)], in_=hbanks[(h, t)][:])
             for h in range(2):
-                nc.scalar.activation(root[:, cols(h)], sq[t][:, cols(h)], ACT.Abs_reciprocal_sqrt, bias=0.5)
+                nc.scalar.activation(sq[:, cols(h)], hbanks[(h, t)][:], ACT.Square)
+            pieces = [cols(0), cols(1)] if t < 1 else [slice(0, S)]
+            for c in pieces:
+                nc.scalar.activation(root[:, c], sq[:, c], ACT.Abs_reciprocal_sqrt, bias=0.5)
             for h in range(2):
-                nc.scalar.activation(inv[:, cols(h)], root[:, cols(h)], ACT.Square)
-            if t > 0:
-                nc.scalar.copy(out=hid[t][:, cols(1)], in_=hbanks[(1, t)][:])
-            for h in range(2):
-                nc.vector.tensor_tensor(f[:, cols(h)], hbanks[(h, t)][:], inv[:, cols(h)], ALU.mult)
-            for h in range(2):
-                nc.vector.tensor_tensor(res[:, cols(h)], f[:].indirect(halves(n3_sb, h)), hid[t][:, cols(h)], ALU.mult)
-                nc.sync.dma_start(out=out_rows[:, t, cols(h)], in_=res[:, cols(h)])
+                if (h, t) in ((1,3,),):
+                    nc.scalar.copy(out=hid[:, cols(h)], in_=hbanks[(h, t)][:])
+                elif t == 0:
+                    nc.vector.tensor_copy(out=hid[:, cols(h)], in_=hbanks[(h, t)][:])
+            for c in pieces:
+                nc.scalar.activation(inv[:, c], root[:, c], ACT.Square)
+            for c in pieces:
+                nc.vector.tensor_tensor(f[:, c], hid[:, c], inv[:, c], ALU.mult)
+            if t < PACK - 1:
+                nc.vector.tensor_tensor(res[:], window[:].indirect(n3_sb[:]), hid[:], ALU.mult)
+                nc.sync.dma_start(out=out_rows[:, t, :], in_=res[:])
+            else:
+                for h in range(2):
+                    nc.vector.tensor_tensor(res[:, cols(h)], window[:].indirect(halves(n3_sb, h)), hid[:, cols(h)], ALU.mult)
+                    nc.sync.dma_start(out=out_rows[:, t, cols(h)], in_=res[:, cols(h)])

from contextlib import ExitStack

import concourse.mybir as mybir

K, T, S, H, N = 512, 2048, 512, 512, 512
FLOPS = 2 * K * H * S + 2 * H * N * S

F32 = mybir.dt.float32
BF16 = mybir.dt.bfloat16
I32 = mybir.dt.int32
U32 = mybir.dt.uint32
U16 = mybir.dt.uint16
U8 = mybir.dt.uint8
FP8X4 = mybir.dt.float8_e4m3fn_x4
ACT = mybir.ActivationFunctionType
ALU = mybir.AluOpType

P = 128
PACK = 4
HALF = S // 2
QUARTER = S // 4
PER_COL = 16
W1_VECTOR_M = 56


def tile_picked_laplace8_none_p_kernel(tc, x_words, x_scales, w1, gn, w2, offs, n1, n2, n3, out):
    nc = tc.nc
    with ExitStack() as ctx:
        keep = ctx.enter_context(tc.tile_pool(name="keep", bufs=1))
        psum = ctx.enter_context(tc.psum_pool(name="psum", bufs=1))

        def sb(name, shape, dtype, tag=None):
            return keep.tile(shape, dtype, name=name, tag=tag or name, align_bytes=64)

        offs_sb = keep.tile([P, S // PER_COL], U16, name="offs_sb")
        n1_sb = keep.tile([P, S // PER_COL], U16, name="n1_sb")
        n2_sb = keep.tile([P, S // PER_COL], U16, name="n2_sb")
        n3_sb = keep.tile([P, S // PER_COL], U16, name="n3_sb")
        xs_all = sb("xs_all", [P, T], U8)
        xw_all = sb("xw_all", [P, T], I32)
        w1_raw = sb("w1_raw", [P, PACK, H], F32)
        w2_raw = sb("w2_raw", [P, PACK, N], F32)
        gn_sb = sb("gn_sb", [P, PACK], F32)

        nc.vector.memset(xs_all[:].bitcast(I32), 0)
        nc.sync.dma_start(offs_sb[:], offs)
        nc.sync.dma_start(out=w1_raw[:], in_=w1.rearrange("(p j) c -> p j c", j=PACK))
        for q in range(4):
            nc.sync.dma_start(out=xs_all[32 * q : 32 * q + 4, :].bitcast(I32), in_=x_scales[0, 4 * q : 4 * q + 4, :].bitcast(I32))
        nc.sync.dma_start(out=xw_all[:], in_=x_words[0].rearrange("p c r -> p (c r)").bitcast(I32))
        nc.sync.dma_start(n2_sb[:], n2)
        nc.sync.dma_start(n1_sb[:], n1)
        nc.sync.dma_start(out=w2_raw[:], in_=w2.rearrange("(p j) c -> p j c", j=PACK))
        nc.sync.dma_start(out=gn_sb[:], in_=gn.rearrange("(p t) o -> p (t o)", t=PACK))
        nc.sync.dma_start(n3_sb[:], n3)

        def halves(tile, h):
            return tile[:, h * (HALF // PER_COL) : (h + 1) * (HALF // PER_COL)]

        def cols(h):
            return slice(h * HALF, (h + 1) * HALF)

        def deal(raw, grouped, vector_m):
            src = raw[:].rearrange("p j (m t) -> p m j t", t=PACK)
            dst = grouped[:].rearrange("p t m j -> p m j t")
            if vector_m > 0:
                nc.vector.tensor_copy(out=dst[:, :vector_m], in_=src[:, :vector_m])
            nc.scalar.copy(out=dst[:, vector_m:], in_=src[:, vector_m:])

        def quantize(grouped_flat, codes, scales):
            nc.vector.quantize_mx(out=codes.bitcast(FP8X4), scales=scales, in_=grouped_flat)

        def product(dst, w_c, w_s, t, rhs_c, rhs_s):
            nc.tensor.matmul_mx(
                out=dst,
                lhsT=w_c[:, t * P : (t + 1) * P].bitcast(FP8X4),
                lhsT_scale=w_s[:, t * P : (t + 1) * P],
                rhs=rhs_c.bitcast(FP8X4),
                rhs_scale=rhs_s,
                start=True,
                stop=True,
            )

        w1_g = sb("w1_g", [P, PACK, P, PACK], BF16)
        w1_c = sb("w1_c", [P, H], U32)
        w1_s = sb("w1_s", [P, H], U8)
        deal(w1_raw, w1_g, W1_VECTOR_M)
        xs = sb("xs", [P, S], U8)
        nc.vector.tensor_copy(xs[:], xs_all[:].indirect(offs_sb[:]))
        quantize(w1_g[:].rearrange("p t m j -> p (t m j)"), w1_c[:], w1_s[:])

        xw = [sb("xw%d" % h, [P, HALF], U32) for h in range(2)]
        for h in range(2):
            nc.vector.tensor_copy(xw[h][:], xw_all[:].bitcast(U32).indirect(halves(offs_sb, h)))

        y = [sb("y%d" % t, [P, S], F32) for t in range(PACK)]
        for pair in range(2):
            for h, t in ((0, 2 * pair), (0, 2 * pair + 1), (1, 2 * pair), (1, 2 * pair + 1)):
                bank = psum.tile([P, HALF], F32, name="ybank%d_%d" % (h, t), tag="bank%d" % (4 * h + t))
                product(bank[:], w1_c, w1_s, t, xw[h][:], xs[:, cols(h)])
                nc.scalar.copy(out=y[t][:, cols(h)], in_=bank[:])

        w2_g = sb("w2_g", [P, PACK, P, PACK], BF16)
        w2_s = sb("w2_s", [P, N], U8)
        deal(w2_raw, w2_g, 0)

        e = [sb("e%d" % h, [P, 2, PACK, QUARTER], F32) for h in range(2)]
        zt = [sb("zt%d" % h, [P, 2, PACK, QUARTER], BF16) for h in range(2)]
        for t in range(PACK):
            first = [sb("first%d_%d" % (t, h), [P, HALF], F32) for h in range(2)]
            diff = sb("diff%d" % t, [P, S], F32)
            dist = sb("dist%d" % t, [P, S], F32)
            for h in range(2):
                nc.vector.tensor_copy(first[h][:], y[t][:].indirect(halves(n2_sb, h)))
            for h in range(2):
                nc.vector.tensor_tensor(diff[:, cols(h)], y[t][:].indirect(halves(n1_sb, h)), first[h][:], ALU.subtract)
            for h in range(2):
                nc.scalar.activation(dist[:, cols(h)], diff[:, cols(h)], ACT.Abs)
                nc.scalar.activation(e[h][:, :, t, :], dist[:, cols(h)].rearrange("p (c n) -> p c n", c=2), ACT.Exp, scale=-1.0)
                if h in (1,):
                    nc.scalar.activation(zt[h][:, :, t, :], e[h][:, :, t, :], ACT.Copy, scale=gn_sb[:, t : t + 1])

        w2_c = sb("w2_c", [P, N], U32, tag="first3_0")
        quantize(w2_g[:].rearrange("p t m j -> p (t m j)"), w2_c[:], w2_s[:])
        warm = sb("warm", [P, 1], F32)
        nc.scalar.activation(warm[:], zt[1][:, 1, PACK - 1, 0:1], ACT.Abs_reciprocal_sqrt, bias=0.5)

        gain = gn_sb[:].unsqueeze(1).unsqueeze(3).to_broadcast([P, QUARTER // 4, PACK, 4])
        hbanks = {}
        for h in range(2):
            z = [sb("z%d_%d" % (h, c), [P, QUARTER, PACK], BF16) for c in range(2)]
            z_c = sb("z_c%d" % h, [P, HALF], U32)
            z_s = sb("z_s%d" % h, [P, HALF], U8)
            for c in range(2):
                if h in (1,):
                    nc.vector.tensor_copy(
                        out=z[c][:].rearrange("p (a i) t -> p a t i", i=4), in_=zt[h][:, c].rearrange("p t (a i) -> p a t i", i=4)
                    )
                    continue
                nc.vector.tensor_tensor(
                    z[c][:].rearrange("p (a i) t -> p a t i", i=4),
                    e[h][:, c].rearrange("p t (a i) -> p a t i", i=4),
                    gain,
                    ALU.mult,
                )
            for c in range(2):
                q = slice(c * QUARTER, (c + 1) * QUARTER)
                quantize(z[c][:].rearrange("p j t -> p (j t)"), z_c[:, q], z_s[:, q])
            for t in range(PACK):
                bank = psum.tile([P, HALF], F32, name="hbank%d_%d" % (h, t), tag="bank%d" % (4 * h + t))
                for c in range(2):
                    q = slice(c * QUARTER, (c + 1) * QUARTER)
                    product(bank[:, q], w2_c, w2_s, t, z_c[:, q], z_s[:, q])
                hbanks[(h, t)] = bank

        fs = []
        out_rows = out.rearrange("(p t) n -> p t n", t=PACK)
        for t in range(PACK):
            hid = sb("hid%d" % t, [P, S], F32)
            sq = sb("sq%d" % t, [P, S], F32)
            root = sb("root%d" % t, [P, S], F32)
            window = sb("window%d" % t, [P, 2 * S], F32)
            f = window[:, :S]
            inv = window[:, S:]
            fs.append(f)
            res = sb("res%d" % t, [P, S], F32)
            for h in range(2):
                if t > 0 and not (h, t) in ((1,3,),):
                    nc.vector.tensor_copy(out=hid[:, cols(h)], in_=hbanks[(h, t)][:])
            for h in range(2):
                nc.scalar.activation(sq[:, cols(h)], hbanks[(h, t)][:], ACT.Square)
            pieces = [cols(0), cols(1)] if t < 1 else [slice(0, S)]
            for c in pieces:
                nc.scalar.activation(root[:, c], sq[:, c], ACT.Abs_reciprocal_sqrt, bias=0.5)
            for h in range(2):
                if (h, t) in ((1,3,),):
                    nc.scalar.copy(out=hid[:, cols(h)], in_=hbanks[(h, t)][:])
                elif t == 0:
                    nc.vector.tensor_copy(out=hid[:, cols(h)], in_=hbanks[(h, t)][:])
            for c in pieces:
                nc.scalar.activation(inv[:, c], root[:, c], ACT.Square)
            for c in pieces:
                nc.vector.tensor_tensor(f[:, c], hid[:, c], inv[:, c], ALU.mult)
            if t < PACK - 1:
                nc.vector.tensor_tensor(res[:], window[:].indirect(n3_sb[:]), hid[:], ALU.mult)
                nc.sync.dma_start(out=out_rows[:, t, :], in_=res[:])
            else:
                for h in range(2):
                    nc.vector.tensor_tensor(res[:, cols(h)], window[:].indirect(halves(n3_sb, h)), hid[:, cols(h)], ALU.mult)
                    nc.sync.dma_start(out=out_rows[:, t, cols(h)], in_=res[:, cols(h)])
